import numpy as np
import ml_dtypes


def mxq(x, axis, fmt="e4m3"):
    dtype, down = {"e4m3": (ml_dtypes.float8_e4m3fn, 7), "e5m2": (ml_dtypes.float8_e5m2, 14)}[fmt]
    v = np.moveaxis(np.asarray(x, np.float32).astype(ml_dtypes.bfloat16).astype(np.float64), axis, -1)
    blocks = v.reshape(v.shape[:-1] + (-1, 32))
    amax = np.abs(blocks).max(-1, keepdims=True)
    byte = np.maximum(np.where(amax > 0, np.frexp(amax)[1] - 1 + 127, 0) - down, 1)
    scale = np.exp2(byte - 127.0)
    codes = (blocks / scale).astype(np.float32).astype(dtype).astype(np.float64)
    return np.moveaxis((codes * scale).reshape(v.shape), -1, axis)


WIDE = False


def mx_kscale(k):
    if not WIDE:
        return np.ones(k)
    levels = np.array([10, -10, 5, -5, 0])
    if k % 512:
        return np.exp2(np.random.permutation(np.resize(levels, k // 32))).repeat(32)
    a = np.empty((k // 512, 16))
    for p in range(k // 512):
        a[p, :8] = np.random.permutation(np.resize(levels, 8))
        for g in range(8):
            far = levels[np.abs(levels - a[p, g]) >= 10]
            a[p, g + 8] = far[np.random.randint(len(far))]
    return np.exp2(a.ravel()).repeat(32)


def f64(x):
    return np.asarray(x).astype(np.float64)


def striped(idx):
    return np.tile(idx.reshape(-1, 16).T, (8, 1)).astype(np.uint16)


def unstriped(offs):
    return offs[:16].T.reshape(-1).astype(np.int64)


def gelu(v):
    return 0.5 * v * (1.0 + np.tanh(np.sqrt(2.0 / np.pi) * (v + 0.044715 * v**3)))


K, T, E, C, H, N = 1536, 512, 8, 128, 512, 256


def by_expert(wq, xq):
    return np.concatenate([wq[e].T @ xq[:, e * C:(e + 1) * C] for e in range(E)], axis=1)


def setup_inputs():
    n = np.random.standard_normal
    s = mx_kscale(K)[:, None]
    u = mx_kscale(H)
    first = np.random.permutation(np.repeat(np.arange(E), T // E))
    second = (first + 1 + np.random.permutation(np.repeat(np.arange(E - 1), -(-T // (E - 1)))[:T])) % E
    while np.bincount(second, minlength=E).max() != T // E:
        load = np.bincount(second, minlength=E); hi, lo = int(load.argmax()), int(load.argmin())
        t = np.flatnonzero((second == hi) & (first != lo))[0]; second[t] = lo
    slot_token = np.empty(E * C, np.int64); pos = np.empty((2, T), np.int64); fill = np.zeros(E, np.int64)
    place = np.stack([np.random.permutation(C) for _ in range(E)])
    for r, deal in enumerate((first, second)):
        for t in np.random.permutation(T):
            e = deal[t]; j = e * C + place[e, fill[e]]; fill[e] += 1; slot_token[j] = t; pos[r, t] = j
    g = np.random.uniform(0.2, 0.8, T)
    return {
        "xT": (n((K, T)) * s).astype(np.float32),
        "w1": (n((E, K, H)) / np.sqrt(K) / s[None] * u[None, None, :]).astype(np.float32),
        "w2": (n((E, H, N)) / np.sqrt(H) / u[None, :, None]).astype(np.float32),
        "gate": np.stack([np.tile(g, (N, 1)), np.tile(1.0 - g, (N, 1))]).astype(np.float32),
        "offs": striped(slot_token),
        "pos1": striped(pos[0]),
        "pos2": striped(pos[1]),
    }


def reference(xT, w1, w2, gate, offs, pos1, pos2):
    idx = unstriped(offs)
    xq = mxq(f64(xT)[:, idx], 0, "e4m3")
    h = gelu(by_expert(mxq(f64(w1), 1, "e4m3"), xq))
    y = by_expert(mxq(f64(w2), 1, "e4m3"), mxq(h, 0, "e4m3"))
    return f64(gate[0]) * y[:, unstriped(pos1)] + f64(gate[1]) * y[:, unstriped(pos2)]

@@ -1,0 +1,276 @@
+from contextlib import ExitStack
+
+import concourse.mybir as mybir
+
+K, T, E, C, H, N = 1536, 512, 8, 128, 512, 256
+P = 128
+PACK = 4
+K_PASS = P * PACK
+PASSES = K // K_PASS
+SLOTS = E * C
+FLOPS = 2 * SLOTS * (K * H + H * N)
+
+F32 = mybir.dt.float32
+BF16 = mybir.dt.bfloat16
+U32 = mybir.dt.uint32
+U16 = mybir.dt.uint16
+U8 = mybir.dt.uint8
+FP8X4 = mybir.dt.float8_e4m3fn_x4
+MULT = mybir.AluOpType.mult
+GELU = mybir.ActivationFunctionType.Gelu_apprx_tanh
+
+AHEAD = 6
+GATHERS = ((0, 384), (384, 768), (768, 1024))
+Y_GROUPS = ((0, 1, 2, 3), (4,), (5, 6), (7,))
+LATE = 5
+
+
+def tile_routed_moe_kernel(tc, xT, w1, w2, gate, offs, pos1, pos2, out):
+    nc = tc.nc
+    with ExitStack() as ctx:
+        lists = ctx.enter_context(tc.tile_pool(name="lists", bufs=1))
+        keep = ctx.enter_context(tc.tile_pool(name="keep", bufs=1))
+        raws = ctx.enter_context(tc.tile_pool(name="raws", bufs=8))
+        groups = ctx.enter_context(tc.tile_pool(name="groups", bufs=5))
+        wcodes = ctx.enter_context(tc.tile_pool(name="wcodes", bufs=8))
+        small = ctx.enter_context(tc.tile_pool(name="small", bufs=3))
+        psum = ctx.enter_context(tc.psum_pool(name="psum", bufs=3))
+        psum_y = ctx.enter_context(tc.psum_pool(name="psum_y", bufs=2))
+
+        offs_sb = lists.tile([P, SLOTS // 16], U16, name="offs_sb")
+        pos1_sb = lists.tile([P, T // 16], U16, name="pos1_sb")
+        pos2_sb = lists.tile([P, T // 16], U16, name="pos2_sb")
+
+        tok_codes = [keep.tile([P, T], U32, name=f"tok_codes{c}", align_bytes=64) for c in range(PASSES)]
+        tok_scales = keep.tile([P, T], U8, name="tok_scales", align_bytes=64)
+        slot_codes = keep.tile([P, PASSES, SLOTS], U32, name="slot_codes", align_bytes=64)
+        slot_scales = keep.tile([P, SLOTS], U8, name="slot_scales", align_bytes=64)
+        y = [keep.tile([P, SLOTS], F32, name=f"y{b}") for b in range(2)]
+        gates = [[keep.tile([P, T], F32, name=f"gate{r}{b}") for b in range(2)] for r in range(2)]
+        warm = keep.tile([P, 8], F32, name="warm")
+
+        nc.gpsimd.memset(tok_scales[:], 0)
+        nc.vector.memset(warm[:], 0.0)
+        nc.scalar.activation(warm[:], warm[:], GELU)
+
+        items = [("x", 0, c) for c in range(PASSES)]
+        for e in range(E):
+            items += [("w1", e, c) for c in range(PASSES)]
+            if e < LATE:
+                items.append(("w2", e, 0))
+        items += [("w2", e, 0) for e in range(LATE, E)]
+        for b in range(2):
+            items += [("gate", r, b) for r in range(2)]
+
+        raw = {}
+        packed = {}
+        codes = {}
+
+        def load(item):
+            kind, e, c = item
+            if kind == "x":
+                t = raws.tile([P, PACK, T], F32, name="raw")
+                src = xT[c * K_PASS : (c + 1) * K_PASS, :].rearrange("(p j) n -> p j n", j=PACK)
+            elif kind == "w1":
+                t = raws.tile([P, PACK, H], F32, name="raw")
+                src = w1[e, c * K_PASS : (c + 1) * K_PASS, :].rearrange("(p j) n -> p j n", j=PACK)
+            elif kind == "w2":
+                t = raws.tile([P, PACK, N], F32, name="raw2", bufs=5)
+                src = w2[e].rearrange("(p j) n -> p j n", j=PACK)
+            else:
+                t = gates[e][c]
+                src = gate[e, c * P : (c + 1) * P, :]
+            nc.sync.dma_start(out=t[:], in_=src)
+            raw[item] = t
+            if item == ("x", 0, 2):
+                nc.sync.dma_start(out=pos1_sb[:], in_=pos1)
+                nc.sync.dma_start(out=pos2_sb[:], in_=pos2)
+
+        def copy_with(engine, dst, src):
+            if engine == "v":
+                nc.vector.tensor_copy(out=dst, in_=src)
+            else:
+                nc.scalar.copy(out=dst, in_=src)
+
+        def interleave(item, shares):
+            kind, e, c = item
+            t = raw.pop(item)
+            if kind == "w1":
+                g = groups.tile([P, H * PACK], BF16, name="group", align_bytes=64)
+                dst = g[:].rearrange("p (t m j) -> p m j t", t=PACK, j=PACK)
+                src = t[:].rearrange("p j (m t) -> p m j t", t=PACK)
+                unit = P
+            else:
+                width = T if kind == "x" else N
+                if kind == "x":
+                    g = groups.tile([P, T * PACK], BF16, name="group", align_bytes=64)
+                else:
+                    g = groups.tile([P, N * PACK], BF16, name="group2", align_bytes=64, bufs=3)
+                dst = g[:].rearrange("p (n i j) -> p n j i", i=4, j=PACK)
+                src = t[:].rearrange("p j (n i) -> p n j i", i=4)
+                unit = width // 4
+            at = 0
+            for engine, part in shares:
+                end = at + part * unit // 8
+                copy_with(engine, dst[:, at:end], src[:, at:end])
+                at = end
+            packed[item] = g
+
+        def quantize(item):
+            kind, e, c = item
+            g = packed.pop(item)
+            if kind == "x":
+                nc.vector.quantize_mx(out=tok_codes[c][:].bitcast(FP8X4), scales=tok_scales[4 * c : P, :], in_=g[:])
+                return
+            width = H if kind == "w1" else N
+            bufs = 8 if kind == "w1" else 4
+            w = wcodes.tile([P, width], U32, name=kind + "_codes", align_bytes=64, bufs=bufs)
+            s = wcodes.tile([P, width], U8, name=kind + "_scales", align_bytes=64, bufs=bufs)
+            nc.vector.quantize_mx(out=w[:].bitcast(FP8X4), scales=s[:], in_=g[:])
+            codes[item] = (w, s)
+
+        def gather_words(c, i):
+            a, b = GATHERS[i]
+            nc.vector.tensor_copy(
+                out=slot_codes[:, c, a:b], in_=tok_codes[c][:].indirect(offs_sb[:, a // 16 : b // 16])
+            )
+
+        def gather_bytes(i):
+            a, b = GATHERS[i]
+            nc.vector.tensor_copy(out=slot_scales[:, a:b], in_=tok_scales[:].indirect(offs_sb[:, a // 16 : b // 16]))
+
+        sums = {}
+        hidden = {}
+        hcodes = {}
+
+        def layer1(e):
+            acc = psum.tile([P, PACK, C], F32, name="acc")
+            ws = [codes.pop(("w1", e, c)) for c in range(PASSES)]
+            cols = slice(e * C, (e + 1) * C)
+            for t in range(PACK):
+                for c in range(PASSES):
+                    w, s = ws[c]
+                    nc.tensor.matmul_mx(
+                        out=acc[:, t, :],
+                        lhsT=w[:, t * P : (t + 1) * P].bitcast(FP8X4),
+                        lhsT_scale=s[:, t * P : (t + 1) * P],
+                        rhs=slot_codes[:, c, cols].bitcast(FP8X4),
+                        rhs_scale=slot_scales[4 * c : P, cols],
+                        start=(c == 0),
+                        stop=(c == PASSES - 1),
+                    )
+            sums[e] = acc
+
+        def activate(e):
+            h = small.tile([P, C, PACK], BF16, name="h", align_bytes=64)
+            nc.scalar.activation(h[:], sums.pop(e)[:].rearrange("p t n -> p n t"), GELU)
+            hidden[e] = h
+
+        def quantize_h(e):
+            h = hidden.pop(e)
+            w = small.tile([P, C], U32, name="h_codes", align_bytes=64)
+            s = small.tile([P, C], U8, name="h_scales", align_bytes=64)
+            nc.vector.quantize_mx(out=w[:].bitcast(FP8X4), scales=s[:], in_=h[:].rearrange("p n t -> p (n t)"))
+            hcodes[e] = (w, s)
+
+        banks = {}
+
+        def layer2(e):
+            group = [g for g in Y_GROUPS if e in g][0]
+            if e == group[0]:
+                for b in range(2):
+                    banks[b] = psum_y.tile([P, 4 * C], F32, name=f"bank{b}")
+            w, s = codes.pop(("w2", e, 0))
+            hw, hs = hcodes.pop(e)
+            at = (e - group[0]) * C
+            for b in range(2):
+                nc.tensor.matmul_mx(
+                    out=banks[b][:, at : at + C],
+                    lhsT=w[:, b * P : (b + 1) * P].bitcast(FP8X4),
+                    lhsT_scale=s[:, b * P : (b + 1) * P],
+                    rhs=hw[:].bitcast(FP8X4),
+                    rhs_scale=hs[:],
+                    start=True,
+                    stop=True,
+                )
+            if e == group[-1]:
+                for b in range(2):
+                    nc.scalar.copy(
+                        out=y[b][:, group[0] * C : (e + 1) * C], in_=banks[b][:, 0 : len(group) * C]
+                    )
+
+        V, S, VS = [("v", 8)], [("s", 8)], [("v", 5), ("s", 3)]
+        loaded = [0]
+
+        def take(item, shares):
+            upto = min(items.index(item) + AHEAD + 1, len(items))
+            for other in items[loaded[0] : upto]:
+                load(other)
+            loaded[0] = max(loaded[0], upto)
+            interleave(item, shares)
+
+        nc.sync.dma_start(out=offs_sb[:], in_=offs)
+        take(("x", 0, 0), V)
+        take(("x", 0, 1), S)
+        quantize(("x", 0, 0))
+        take(("x", 0, 2), VS)
+        gather_words(0, 0)
+        quantize(("x", 0, 1))
+        quantize(("x", 0, 2))
+        gather_words(1, 0)
+        gather_words(2, 0)
+        gather_bytes(0)
+
+        later = []
+        for i in (1, 2):
+            later += [lambda c=c, i=i: gather_words(c, i) for c in range(PASSES)]
+            later.append(lambda i=i: gather_bytes(i))
+
+        for e in range(E):
+            last = e == E - 1
+            take(("w1", e, 0), S)
+            if e > 0:
+                activate(e - 1)
+            take(("w1", e, 1), V)
+            if later:
+                later.pop(0)()
+            quantize(("w1", e, 0))
+            quantize(("w1", e, 1))
+            if e > 0:
+                quantize_h(e - 1)
+                if e <= LATE:
+                    layer2(e - 1)
+            take(("w1", e, 2), VS if last else S)
+            if e < LATE:
+                take(("w2", e, 0), V)
+                quantize(("w2", e, 0))
+            if later:
+                later.pop(0)()
+            quantize(("w1", e, 2))
+            layer1(e)
+
+        take(("w2", 5, 0), S)
+        take(("w2", 6, 0), V)
+        activate(7)
+        quantize(("w2", 5, 0))
+        layer2(5)
+        take(("w2", 7, 0), V)
+        quantize(("w2", 6, 0))
+        layer2(6)
+        quantize_h(7)
+        quantize(("w2", 7, 0))
+        layer2(7)
+        for other in items[loaded[0] :]:
+            load(other)
+
+        for b in range(2):
+            parts = []
+            for r, plist in ((0, pos1_sb), (1, pos2_sb)):
+                part = small.tile([P, T], F32, name=f"part{r}", bufs=2)
+                nc.vector.tensor_tensor(part[:], y[b][:].indirect(plist[:]), gates[r][b][:], MULT)
+                parts.append(part)
+            res = small.tile([P, T], F32, name="res", bufs=2)
+            for a in range(0, T, T // 2):
+                half = slice(a, a + T // 2)
+                nc.vector.tensor_add(res[:, half], parts[0][:, half], parts[1][:, half])
+                nc.sync.dma_start(out=out[b * P : (b + 1) * P, half], in_=res[:, half])

@@ -19,10 +19,10 @@ FP8X4 = mybir.dt.float8_e4m3fn_x4
 MULT = mybir.AluOpType.mult
 GELU = mybir.ActivationFunctionType.Gelu_apprx_tanh
 
-AHEAD = 6
+AHEAD = 7
 GATHERS = ((0, 384), (384, 768), (768, 1024))
-Y_GROUPS = ((0, 1, 2, 3), (4,), (5, 6), (7,))
-LATE = 5
+W2_LOADS = ((0, 1), (2, 3), (4, 5), (6,), (7,))
+Y_GROUPS = ((0, 1, 2, 3), (4, 5), (6, 7))
 
 
 def tile_routed_moe_kernel(tc, xT, w1, w2, gate, offs, pos1, pos2, out):
@@ -30,9 +30,9 @@ def tile_routed_moe_kernel(tc, xT, w1, w2, gate, offs, pos1, pos2, out):
     with ExitStack() as ctx:
         lists = ctx.enter_context(tc.tile_pool(name="lists", bufs=1))
         keep = ctx.enter_context(tc.tile_pool(name="keep", bufs=1))
-        raws = ctx.enter_context(tc.tile_pool(name="raws", bufs=8))
-        groups = ctx.enter_context(tc.tile_pool(name="groups", bufs=5))
-        wcodes = ctx.enter_context(tc.tile_pool(name="wcodes", bufs=8))
+        raws = ctx.enter_context(tc.tile_pool(name="raws", bufs=10))
+        groups = ctx.enter_context(tc.tile_pool(name="groups", bufs=3))
+        wcodes = ctx.enter_context(tc.tile_pool(name="wcodes", bufs=3))
         small = ctx.enter_context(tc.tile_pool(name="small", bufs=3))
         psum = ctx.enter_context(tc.psum_pool(name="psum", bufs=3))
         psum_y = ctx.enter_context(tc.psum_pool(name="psum_y", bufs=2))
@@ -56,78 +56,90 @@ def tile_routed_moe_kernel(tc, xT, w1, w2, gate, offs, pos1, pos2, out):
         items = [("x", 0, c) for c in range(PASSES)]
         for e in range(E):
             items += [("w1", e, c) for c in range(PASSES)]
-            if e < LATE:
-                items.append(("w2", e, 0))
-        items += [("w2", e, 0) for e in range(LATE, E)]
+            if e == 1:
+                items.append(("w2", 0, 0))
+        items += [("w2", i, 0) for i in range(1, len(W2_LOADS))]
         for b in range(2):
             items += [("gate", r, b) for r in range(2)]
 
         raw = {}
-        packed = {}
-        codes = {}
+        loaded = [0]
 
         def load(item):
             kind, e, c = item
+            rows = slice(c * K_PASS, (c + 1) * K_PASS)
             if kind == "x":
                 t = raws.tile([P, PACK, T], F32, name="raw")
-                src = xT[c * K_PASS : (c + 1) * K_PASS, :].rearrange("(p j) n -> p j n", j=PACK)
+                nc.sync.dma_start(out=t[:], in_=xT[rows, :].rearrange("(p j) n -> p j n", j=PACK))
             elif kind == "w1":
                 t = raws.tile([P, PACK, H], F32, name="raw")
-                src = w1[e, c * K_PASS : (c + 1) * K_PASS, :].rearrange("(p j) n -> p j n", j=PACK)
+                nc.sync.dma_start(out=t[:], in_=w1[e, rows, :].rearrange("(p j) n -> p j n", j=PACK))
             elif kind == "w2":
-                t = raws.tile([P, PACK, N], F32, name="raw2", bufs=5)
-                src = w2[e].rearrange("(p j) n -> p j n", j=PACK)
+                which = W2_LOADS[e]
+                if len(which) == 2:
+                    t = raws.tile([P, 2, PACK, N], F32, name="raw")
+                    src = w2[which[0] : which[0] + 2].rearrange("x (p j) n -> p x j n", j=PACK)
+                else:
+                    t = raws.tile([P, 1, PACK, N], F32, name="raw_single", bufs=2)
+                    src = w2[which[0] : which[0] + 1].rearrange("x (p j) n -> p x j n", j=PACK)
+                nc.sync.dma_start(out=t[:], in_=src)
             else:
                 t = gates[e][c]
-                src = gate[e, c * P : (c + 1) * P, :]
-            nc.sync.dma_start(out=t[:], in_=src)
+                nc.sync.dma_start(out=t[:], in_=gate[e, c * P : (c + 1) * P, :])
             raw[item] = t
             if item == ("x", 0, 2):
                 nc.sync.dma_start(out=pos1_sb[:], in_=pos1)
                 nc.sync.dma_start(out=pos2_sb[:], in_=pos2)
 
-        def copy_with(engine, dst, src):
-            if engine == "v":
-                nc.vector.tensor_copy(out=dst, in_=src)
-            else:
-                nc.scalar.copy(out=dst, in_=src)
+        def take(item):
+            upto = min(items.index(item) + AHEAD + 1, len(items))
+            for other in items[loaded[0] : upto]:
+                load(other)
+            loaded[0] = max(loaded[0], upto)
+            return raw.pop(item)
 
-        def interleave(item, shares):
-            kind, e, c = item
-            t = raw.pop(item)
-            if kind == "w1":
-                g = groups.tile([P, H * PACK], BF16, name="group", align_bytes=64)
-                dst = g[:].rearrange("p (t m j) -> p m j t", t=PACK, j=PACK)
-                src = t[:].rearrange("p j (m t) -> p m j t", t=PACK)
-                unit = P
-            else:
-                width = T if kind == "x" else N
-                if kind == "x":
-                    g = groups.tile([P, T * PACK], BF16, name="group", align_bytes=64)
-                else:
-                    g = groups.tile([P, N * PACK], BF16, name="group2", align_bytes=64, bufs=3)
-                dst = g[:].rearrange("p (n i j) -> p n j i", i=4, j=PACK)
-                src = t[:].rearrange("p j (n i) -> p n j i", i=4)
-                unit = width // 4
+        def share(dst, src, units, shares):
             at = 0
             for engine, part in shares:
-                end = at + part * unit // 8
-                copy_with(engine, dst[:, at:end], src[:, at:end])
+                end = at + part * units // 8
+                if engine == "v":
+                    nc.vector.tensor_copy(out=dst[:, at:end], in_=src[:, at:end])
+                else:
+                    nc.scalar.copy(out=dst[:, at:end], in_=src[:, at:end])
                 at = end
-            packed[item] = g
 
-        def quantize(item):
-            kind, e, c = item
-            g = packed.pop(item)
-            if kind == "x":
-                nc.vector.quantize_mx(out=tok_codes[c][:].bitcast(FP8X4), scales=tok_scales[4 * c : P, :], in_=g[:])
-                return
-            width = H if kind == "w1" else N
-            bufs = 8 if kind == "w1" else 4
-            w = wcodes.tile([P, width], U32, name=kind + "_codes", align_bytes=64, bufs=bufs)
-            s = wcodes.tile([P, width], U8, name=kind + "_scales", align_bytes=64, bufs=bufs)
+        def plain(group, raw_tile, width, shares):
+            share(
+                group.rearrange("p (n i j) -> p n j i", i=4, j=PACK),
+                raw_tile.rearrange("p j (n i) -> p n j i", i=4),
+                width // 4,
+                shares,
+            )
+
+        def permuted(group, raw_tile, shares):
+            share(
+                group.rearrange("p (t m j) -> p m j t", t=PACK, j=PACK),
+                raw_tile.rearrange("p j (m t) -> p m j t", t=PACK),
+                P,
+                shares,
+            )
+
+        V, S, VS = [("v", 8)], [("s", 8)], [("v", 5), ("s", 3)]
+
+        def take_x(c, shares):
+            t = take(("x", 0, c))
+            g = groups.tile([P, T * PACK], BF16, name="group", align_bytes=64, bufs=4)
+            plain(g[:], t[:], T, shares)
+            return g
+
+        def quantize_x(c, g):
+            nc.vector.quantize_mx(out=tok_codes[c][:].bitcast(FP8X4), scales=tok_scales[4 * c : P, :], in_=g[:])
+
+        def quantize(g, width, name, bufs):
+            w = wcodes.tile([P, width], U32, name=name + "_codes", align_bytes=64, bufs=bufs)
+            s = wcodes.tile([P, width], U8, name=name + "_scales", align_bytes=64, bufs=bufs)
             nc.vector.quantize_mx(out=w[:].bitcast(FP8X4), scales=s[:], in_=g[:])
-            codes[item] = (w, s)
+            return w, s
 
         def gather_words(c, i):
             a, b = GATHERS[i]
@@ -139,21 +151,42 @@ def tile_routed_moe_kernel(tc, xT, w1, w2, gate, offs, pos1, pos2, out):
             a, b = GATHERS[i]
             nc.vector.tensor_copy(out=slot_scales[:, a:b], in_=tok_scales[:].indirect(offs_sb[:, a // 16 : b // 16]))
 
+        w2_codes = {}
+
+        def take_w2(i, shares):
+            which = W2_LOADS[i]
+            t = take(("w2", i, 0))
+            width = len(which) * N
+            if len(which) == 2:
+                g = groups.tile([P, width * PACK], BF16, name="group", align_bytes=64, bufs=4)
+            else:
+                g = groups.tile([P, width * PACK], BF16, name="group_single", align_bytes=64, bufs=2)
+            for x in range(len(which)):
+                plain(g[:, x * N * PACK : (x + 1) * N * PACK], t[:, x], N, shares)
+            return g
+
+        def quantize_w2(i, g):
+            which = W2_LOADS[i]
+            pair = quantize(g, len(which) * N, "w2pair" if len(which) == 2 else "w2single", 3)
+            for x, e in enumerate(which):
+                w2_codes[e] = (pair, x * N)
+
         sums = {}
         hidden = {}
         hcodes = {}
+        banks = {}
 
-        def layer1(e):
+        def layer1(e, w01, w_2):
             acc = psum.tile([P, PACK, C], F32, name="acc")
-            ws = [codes.pop(("w1", e, c)) for c in range(PASSES)]
             cols = slice(e * C, (e + 1) * C)
             for t in range(PACK):
                 for c in range(PASSES):
-                    w, s = ws[c]
+                    w, s = w01 if c < 2 else w_2
+                    lo = (c % 2) * H + t * P
                     nc.tensor.matmul_mx(
                         out=acc[:, t, :],
-                        lhsT=w[:, t * P : (t + 1) * P].bitcast(FP8X4),
-                        lhsT_scale=s[:, t * P : (t + 1) * P],
+                        lhsT=w[:, lo : lo + P].bitcast(FP8X4),
+                        lhsT_scale=s[:, lo : lo + P],
                         rhs=slot_codes[:, c, cols].bitcast(FP8X4),
                         rhs_scale=slot_scales[4 * c : P, cols],
                         start=(c == 0),
@@ -168,26 +201,24 @@ def tile_routed_moe_kernel(tc, xT, w1, w2, gate, offs, pos1, pos2, out):
 
         def quantize_h(e):
             h = hidden.pop(e)
-            w = small.tile([P, C], U32, name="h_codes", align_bytes=64)
-            s = small.tile([P, C], U8, name="h_scales", align_bytes=64)
+            w = small.tile([P, C], U32, name="h_codes", align_bytes=64, bufs=8)
+            s = small.tile([P, C], U8, name="h_scales", align_bytes=64, bufs=8)
             nc.vector.quantize_mx(out=w[:].bitcast(FP8X4), scales=s[:], in_=h[:].rearrange("p n t -> p (n t)"))
             hcodes[e] = (w, s)
 
-        banks = {}
-
         def layer2(e):
             group = [g for g in Y_GROUPS if e in g][0]
-            if e == group[0]:
-                for b in range(2):
-                    banks[b] = psum_y.tile([P, 4 * C], F32, name=f"bank{b}")
-            w, s = codes.pop(("w2", e, 0))
             hw, hs = hcodes.pop(e)
+            (w, s), lo = w2_codes.pop(e)
             at = (e - group[0]) * C
             for b in range(2):
+                if e == group[0]:
+                    banks[b] = psum_y.tile([P, 4 * C], F32, name=f"bank{b}")
+                cols = slice(lo + b * P, lo + (b + 1) * P)
                 nc.tensor.matmul_mx(
                     out=banks[b][:, at : at + C],
-                    lhsT=w[:, b * P : (b + 1) * P].bitcast(FP8X4),
-                    lhsT_scale=s[:, b * P : (b + 1) * P],
+                    lhsT=w[:, cols].bitcast(FP8X4),
+                    lhsT_scale=s[:, cols],
                     rhs=hw[:].bitcast(FP8X4),
                     rhs_scale=hs[:],
                     start=True,
@@ -195,28 +226,28 @@ def tile_routed_moe_kernel(tc, xT, w1, w2, gate, offs, pos1, pos2, out):
                 )
             if e == group[-1]:
                 for b in range(2):
-                    nc.scalar.copy(
-                        out=y[b][:, group[0] * C : (e + 1) * C], in_=banks[b][:, 0 : len(group) * C]
-                    )
+                    nc.scalar.copy(out=y[b][:, group[0] * C : (e + 1) * C], in_=banks[b][:, 0 : len(group) * C])
 
-        V, S, VS = [("v", 8)], [("s", 8)], [("v", 5), ("s", 3)]
-        loaded = [0]
-
-        def take(item, shares):
-            upto = min(items.index(item) + AHEAD + 1, len(items))
-            for other in items[loaded[0] : upto]:
-                load(other)
-            loaded[0] = max(loaded[0], upto)
-            interleave(item, shares)
+        def combine(b):
+            parts = []
+            for r, plist in ((0, pos1_sb), (1, pos2_sb)):
+                part = small.tile([P, T], F32, name=f"part{r}", bufs=2)
+                nc.vector.tensor_tensor(part[:], y[b][:].indirect(plist[:]), gates[r][b][:], MULT)
+                parts.append(part)
+            res = small.tile([P, T], F32, name="res", bufs=2)
+            for a in range(0, T, T // 2):
+                half = slice(a, a + T // 2)
+                nc.vector.tensor_add(res[:, half], parts[0][:, half], parts[1][:, half])
+                nc.sync.dma_start(out=out[b * P : (b + 1) * P, half], in_=res[:, half])
 
         nc.sync.dma_start(out=offs_sb[:], in_=offs)
-        take(("x", 0, 0), V)
-        take(("x", 0, 1), S)
-        quantize(("x", 0, 0))
-        take(("x", 0, 2), VS)
+        g0 = take_x(0, V)
+        g1 = take_x(1, S)
+        quantize_x(0, g0)
+        g2 = take_x(2, VS)
         gather_words(0, 0)
-        quantize(("x", 0, 1))
-        quantize(("x", 0, 2))
+        quantize_x(1, g1)
+        quantize_x(2, g2)
         gather_words(1, 0)
         gather_words(2, 0)
         gather_bytes(0)
@@ -228,49 +259,44 @@ def tile_routed_moe_kernel(tc, xT, w1, w2, gate, offs, pos1, pos2, out):
 
         for e in range(E):
             last = e == E - 1
-            take(("w1", e, 0), S)
+            g01 = groups.tile([P, 2 * H * PACK], BF16, name="group01", align_bytes=64, bufs=3)
+            permuted(g01[:, 0 : H * PACK], take(("w1", e, 0))[:], S)
             if e > 0:
                 activate(e - 1)
-            take(("w1", e, 1), V)
+            permuted(g01[:, H * PACK :], take(("w1", e, 1))[:], V)
             if later:
                 later.pop(0)()
-            quantize(("w1", e, 0))
-            quantize(("w1", e, 1))
+            w01 = quantize(g01, 2 * H, "w01", 3)
             if e > 0:
                 quantize_h(e - 1)
-                if e <= LATE:
-                    layer2(e - 1)
-            take(("w1", e, 2), VS if last else S)
-            if e < LATE:
-                take(("w2", e, 0), V)
-                quantize(("w2", e, 0))
+            if e == 2:
+                layer2(0)
+                layer2(1)
+            g_2 = groups.tile([P, H * PACK], BF16, name="group", align_bytes=64, bufs=4)
+            permuted(g_2[:], take(("w1", e, 2))[:], VS if last else S)
+            if e == 1:
+                gw = take_w2(0, V)
+                quantize_w2(0, gw)
             if later:
                 later.pop(0)()
-            quantize(("w1", e, 2))
-            layer1(e)
+            w_2 = quantize(g_2, H, "w_2", 3)
+            layer1(e, w01, w_2)
 
-        take(("w2", 5, 0), S)
-        take(("w2", 6, 0), V)
+        ga = take_w2(1, VS)
+        gb = take_w2(2, V)
+        quantize_w2(1, ga)
+        layer2(2)
+        layer2(3)
         activate(7)
-        quantize(("w2", 5, 0))
-        layer2(5)
-        take(("w2", 7, 0), V)
-        quantize(("w2", 6, 0))
-        layer2(6)
+        quantize_w2(2, gb)
         quantize_h(7)
-        quantize(("w2", 7, 0))
+        layer2(4)
+        layer2(5)
+        gb = take_w2(3, S)
+        gc = take_w2(4, V)
+        quantize_w2(3, gb)
+        layer2(6)
+        quantize_w2(4, gc)
         layer2(7)
-        for other in items[loaded[0] :]:
-            load(other)
-
         for b in range(2):
-            parts = []
-            for r, plist in ((0, pos1_sb), (1, pos2_sb)):
-                part = small.tile([P, T], F32, name=f"part{r}", bufs=2)
-                nc.vector.tensor_tensor(part[:], y[b][:].indirect(plist[:]), gates[r][b][:], MULT)
-                parts.append(part)
-            res = small.tile([P, T], F32, name="res", bufs=2)
-            for a in range(0, T, T // 2):
-                half = slice(a, a + T // 2)
-                nc.vector.tensor_add(res[:, half], parts[0][:, half], parts[1][:, half])
-                nc.sync.dma_start(out=out[b * P : (b + 1) * P, half], in_=res[:, half])
+            combine(b)

@@ -19,10 +19,12 @@ FP8X4 = mybir.dt.float8_e4m3fn_x4
 MULT = mybir.AluOpType.mult
 GELU = mybir.ActivationFunctionType.Gelu_apprx_tanh
 
-AHEAD = 7
-GATHERS = ((0, 384), (384, 768), (768, 1024))
-W2_LOADS = ((0, 1), (2, 3), (4, 5), (6,), (7,))
-Y_GROUPS = ((0, 1, 2, 3), (4, 5), (6, 7))
+CHUNK = 256
+W1_LOADS = tuple(((0,), (1,), (2,)) for e in range(E))
+W2_PAIRS = ((0, 1), (2, 3), (4, 5))
+RINGS = {1: 10}
+IN_FLIGHT = 8
+Y_GROUPS = ((0, 1, 2, 3), (4, 5), (6,), (7,))
 
 
 def tile_routed_moe_kernel(tc, xT, w1, w2, gate, offs, pos1, pos2, out):
@@ -30,9 +32,10 @@ def tile_routed_moe_kernel(tc, xT, w1, w2, gate, offs, pos1, pos2, out):
     with ExitStack() as ctx:
         lists = ctx.enter_context(tc.tile_pool(name="lists", bufs=1))
         keep = ctx.enter_context(tc.tile_pool(name="keep", bufs=1))
-        raws = ctx.enter_context(tc.tile_pool(name="raws", bufs=10))
+        raws = ctx.enter_context(tc.tile_pool(name="raws", bufs=2))
         groups = ctx.enter_context(tc.tile_pool(name="groups", bufs=3))
         wcodes = ctx.enter_context(tc.tile_pool(name="wcodes", bufs=3))
+        slots = ctx.enter_context(tc.tile_pool(name="slots", bufs=2))
         small = ctx.enter_context(tc.tile_pool(name="small", bufs=3))
         psum = ctx.enter_context(tc.psum_pool(name="psum", bufs=3))
         psum_y = ctx.enter_context(tc.psum_pool(name="psum_y", bufs=2))
@@ -43,60 +46,65 @@ def tile_routed_moe_kernel(tc, xT, w1, w2, gate, offs, pos1, pos2, out):
 
         tok_codes = [keep.tile([P, T], U32, name=f"tok_codes{c}", align_bytes=64) for c in range(PASSES)]
         tok_scales = keep.tile([P, T], U8, name="tok_scales", align_bytes=64)
-        slot_codes = keep.tile([P, PASSES, SLOTS], U32, name="slot_codes", align_bytes=64)
-        slot_scales = keep.tile([P, SLOTS], U8, name="slot_scales", align_bytes=64)
         y = [keep.tile([P, SLOTS], F32, name=f"y{b}") for b in range(2)]
-        gates = [[keep.tile([P, T], F32, name=f"gate{r}{b}") for b in range(2)] for r in range(2)]
+        gates = [keep.tile([P, 2, T], F32, name=f"gate{b}") for b in range(2)]
         warm = keep.tile([P, 8], F32, name="warm")
 
         nc.gpsimd.memset(tok_scales[:], 0)
         nc.vector.memset(warm[:], 0.0)
         nc.scalar.activation(warm[:], warm[:], GELU)
 
-        items = [("x", 0, c) for c in range(PASSES)]
+        items = [("x", c, 1) for c in range(PASSES)]
         for e in range(E):
-            items += [("w1", e, c) for c in range(PASSES)]
+            items += [("w1", (e, group[0]), len(group)) for group in W1_LOADS[e]]
             if e == 1:
-                items.append(("w2", 0, 0))
-        items += [("w2", i, 0) for i in range(1, len(W2_LOADS))]
-        for b in range(2):
-            items += [("gate", r, b) for r in range(2)]
+                items.append(("w2", 0, 1))
+        items += [("w2", 1, 1), ("w2", 2, 1)]
+        items += [("late", e, 1) for e in (E - 2, E - 1)]
+        items += [("gate", b, 1) for b in range(2)]
 
         raw = {}
-        loaded = [0]
+        room = dict(RINGS)
+        room["late"] = 2
+        room["gate"] = 2
+
+        def ring_of(item):
+            return item[0] if item[0] in ("late", "gate") else item[2]
 
         def load(item):
-            kind, e, c = item
-            rows = slice(c * K_PASS, (c + 1) * K_PASS)
+            kind, which, size = item
             if kind == "x":
-                t = raws.tile([P, PACK, T], F32, name="raw")
-                nc.sync.dma_start(out=t[:], in_=xT[rows, :].rearrange("(p j) n -> p j n", j=PACK))
+                t = raws.tile([P, 1, PACK, T], F32, name="raw1", bufs=RINGS[1])
+                src = xT[which * K_PASS : (which + 1) * K_PASS, :].rearrange("(g p j) n -> p g j n", p=P, j=PACK)
             elif kind == "w1":
-                t = raws.tile([P, PACK, H], F32, name="raw")
-                nc.sync.dma_start(out=t[:], in_=w1[e, rows, :].rearrange("(p j) n -> p j n", j=PACK))
+                e, c = which
+                t = raws.tile([P, size, PACK, H], F32, name=f"raw{size}", bufs=RINGS[size])
+                src = w1[e, c * K_PASS : (c + size) * K_PASS, :].rearrange("(g p j) n -> p g j n", p=P, j=PACK)
             elif kind == "w2":
-                which = W2_LOADS[e]
-                if len(which) == 2:
-                    t = raws.tile([P, 2, PACK, N], F32, name="raw")
-                    src = w2[which[0] : which[0] + 2].rearrange("x (p j) n -> p x j n", j=PACK)
-                else:
-                    t = raws.tile([P, 1, PACK, N], F32, name="raw_single", bufs=2)
-                    src = w2[which[0] : which[0] + 1].rearrange("x (p j) n -> p x j n", j=PACK)
-                nc.sync.dma_start(out=t[:], in_=src)
+                t = raws.tile([P, 2, PACK, N], F32, name="raw1", bufs=RINGS[1])
+                src = w2[2 * which : 2 * which + 2].rearrange("x (p j) n -> p x j n", j=PACK)
+            elif kind == "late":
+                t = raws.tile([P, PACK, N], F32, name="raw_late")
+                src = w2[which].rearrange("(p j) n -> p j n", j=PACK)
             else:
-                t = gates[e][c]
-                nc.sync.dma_start(out=t[:], in_=gate[e, c * P : (c + 1) * P, :])
+                t = gates[which]
+                src = gate[:, which * P : (which + 1) * P, :].rearrange("r n t -> n r t")
+            nc.sync.dma_start(out=t[:], in_=src)
             raw[item] = t
-            if item == ("x", 0, 2):
+            if item == ("x", PASSES - 1, 1):
                 nc.sync.dma_start(out=pos1_sb[:], in_=pos1)
                 nc.sync.dma_start(out=pos2_sb[:], in_=pos2)
 
-        def take(item):
-            upto = min(items.index(item) + AHEAD + 1, len(items))
-            for other in items[loaded[0] : upto]:
-                load(other)
-            loaded[0] = max(loaded[0], upto)
-            return raw.pop(item)
+        def pump():
+            while items and room[ring_of(items[0])] > 0 and len(raw) < IN_FLIGHT:
+                item = items.pop(0)
+                room[ring_of(item)] -= 1
+                load(item)
+
+        def done(item):
+            raw.pop(item)
+            room[ring_of(item)] += 1
+            pump()
 
         def share(dst, src, units, shares):
             at = 0
@@ -124,12 +132,13 @@ def tile_routed_moe_kernel(tc, xT, w1, w2, gate, offs, pos1, pos2, out):
                 shares,
             )
 
-        V, S, VS = [("v", 8)], [("s", 8)], [("v", 5), ("s", 3)]
+        V, S, VS, SV = [("v", 8)], [("s", 8)], [("v", 5), ("s", 3)], [("v", 3), ("s", 5)]
 
         def take_x(c, shares):
-            t = take(("x", 0, c))
+            item = ("x", c, 1)
             g = groups.tile([P, T * PACK], BF16, name="group", align_bytes=64, bufs=4)
-            plain(g[:], t[:], T, shares)
+            plain(g[:], raw[item][:, 0], T, shares)
+            done(item)
             return g
 
         def quantize_x(c, g):
@@ -141,35 +150,55 @@ def tile_routed_moe_kernel(tc, xT, w1, w2, gate, offs, pos1, pos2, out):
             nc.vector.quantize_mx(out=w[:].bitcast(FP8X4), scales=s[:], in_=g[:])
             return w, s
 
-        def gather_words(c, i):
-            a, b = GATHERS[i]
-            nc.vector.tensor_copy(
-                out=slot_codes[:, c, a:b], in_=tok_codes[c][:].indirect(offs_sb[:, a // 16 : b // 16])
-            )
+        slot_words = {}
+        slot_bytes = {}
+
+        def gather_words(i, c):
+            if c == 0:
+                slot_words[i] = slots.tile([P, PASSES, CHUNK], U32, name="slot_words", align_bytes=64)
+            at = offs_sb[:, i * CHUNK // 16 : (i + 1) * CHUNK // 16]
+            nc.vector.tensor_copy(out=slot_words[i][:, c, :], in_=tok_codes[c][:].indirect(at))
 
         def gather_bytes(i):
-            a, b = GATHERS[i]
-            nc.vector.tensor_copy(out=slot_scales[:, a:b], in_=tok_scales[:].indirect(offs_sb[:, a // 16 : b // 16]))
+            slot_bytes[i] = slots.tile([P, CHUNK], U8, name="slot_bytes", align_bytes=64)
+            at = offs_sb[:, i * CHUNK // 16 : (i + 1) * CHUNK // 16]
+            nc.vector.tensor_copy(out=slot_bytes[i][:], in_=tok_scales[:].indirect(at))
+
+        def gather_some(i, part):
+            if part == 0:
+                gather_words(i, 0)
+                gather_words(i, 1)
+            else:
+                gather_words(i, 2)
+                gather_bytes(i)
 
         w2_codes = {}
 
         def take_w2(i, shares):
-            which = W2_LOADS[i]
-            t = take(("w2", i, 0))
-            width = len(which) * N
-            if len(which) == 2:
-                g = groups.tile([P, width * PACK], BF16, name="group", align_bytes=64, bufs=4)
-            else:
-                g = groups.tile([P, width * PACK], BF16, name="group_single", align_bytes=64, bufs=2)
-            for x in range(len(which)):
-                plain(g[:, x * N * PACK : (x + 1) * N * PACK], t[:, x], N, shares)
+            item = ("w2", i, 1)
+            g = groups.tile([P, 2 * N * PACK], BF16, name="group", align_bytes=64, bufs=4)
+            for x in range(2):
+                plain(g[:, x * N * PACK : (x + 1) * N * PACK], raw[item][:, x], N, shares)
+            done(item)
             return g
 
         def quantize_w2(i, g):
-            which = W2_LOADS[i]
-            pair = quantize(g, len(which) * N, "w2pair" if len(which) == 2 else "w2single", 3)
-            for x, e in enumerate(which):
-                w2_codes[e] = (pair, x * N)
+            pair = quantize(g, 2 * N, "w2pair", 3)
+            for x, e in enumerate(W2_PAIRS[i]):
+                w2_codes[e] = [(pair, x * N + b * P) for b in range(2)]
+
+        def take_late(e, shares):
+            item = ("late", e, 1)
+            halves = []
+            for b in range(2):
+                g = groups.tile([P, P * PACK], BF16, name="group_half", align_bytes=64, bufs=4)
+                plain(g[:], raw[item][:, :, b * P : (b + 1) * P], P, shares[b])
+                halves.append(g)
+            done(item)
+            return halves
+
+        def quantize_late(e, halves):
+            w2_codes[e] = [(quantize(g, P, "w2half", 4), 0) for g in halves]
 
         sums = {}
         hidden = {}
@@ -178,7 +207,7 @@ def tile_routed_moe_kernel(tc, xT, w1, w2, gate, offs, pos1, pos2, out):
 
         def layer1(e, w01, w_2):
             acc = psum.tile([P, PACK, C], F32, name="acc")
-            cols = slice(e * C, (e + 1) * C)
+            cols = slice((e % 2) * C, (e % 2 + 1) * C)
             for t in range(PACK):
                 for c in range(PASSES):
                     w, s = w01 if c < 2 else w_2
@@ -187,8 +216,8 @@ def tile_routed_moe_kernel(tc, xT, w1, w2, gate, offs, pos1, pos2, out):
                         out=acc[:, t, :],
                         lhsT=w[:, lo : lo + P].bitcast(FP8X4),
                         lhsT_scale=s[:, lo : lo + P],
-                        rhs=slot_codes[:, c, cols].bitcast(FP8X4),
-                        rhs_scale=slot_scales[4 * c : P, cols],
+                        rhs=slot_words[e // 2][:, c, cols].bitcast(FP8X4),
+                        rhs_scale=slot_bytes[e // 2][4 * c : P, cols],
                         start=(c == 0),
                         stop=(c == PASSES - 1),
                     )
@@ -208,39 +237,39 @@ def tile_routed_moe_kernel(tc, xT, w1, w2, gate, offs, pos1, pos2, out):
 
         def layer2(e):
             group = [g for g in Y_GROUPS if e in g][0]
-            hw, hs = hcodes.pop(e)
-            (w, s), lo = w2_codes.pop(e)
+            hw, hs = hcodes[e]
             at = (e - group[0]) * C
             for b in range(2):
                 if e == group[0]:
                     banks[b] = psum_y.tile([P, 4 * C], F32, name=f"bank{b}")
-                cols = slice(lo + b * P, lo + (b + 1) * P)
+                (w, s), lo = w2_codes[e][b]
                 nc.tensor.matmul_mx(
                     out=banks[b][:, at : at + C],
-                    lhsT=w[:, cols].bitcast(FP8X4),
-                    lhsT_scale=s[:, cols],
+                    lhsT=w[:, lo : lo + P].bitcast(FP8X4),
+                    lhsT_scale=s[:, lo : lo + P],
                     rhs=hw[:].bitcast(FP8X4),
                     rhs_scale=hs[:],
                     start=True,
                     stop=True,
                 )
-            if e == group[-1]:
-                for b in range(2):
+                if e == group[-1]:
                     nc.scalar.copy(out=y[b][:, group[0] * C : (e + 1) * C], in_=banks[b][:, 0 : len(group) * C])
 
         def combine(b):
             parts = []
             for r, plist in ((0, pos1_sb), (1, pos2_sb)):
                 part = small.tile([P, T], F32, name=f"part{r}", bufs=2)
-                nc.vector.tensor_tensor(part[:], y[b][:].indirect(plist[:]), gates[r][b][:], MULT)
+                nc.vector.tensor_tensor(part[:], y[b][:].indirect(plist[:]), gates[b][:, r, :], MULT)
                 parts.append(part)
             res = small.tile([P, T], F32, name="res", bufs=2)
-            for a in range(0, T, T // 2):
-                half = slice(a, a + T // 2)
-                nc.vector.tensor_add(res[:, half], parts[0][:, half], parts[1][:, half])
-                nc.sync.dma_start(out=out[b * P : (b + 1) * P, half], in_=res[:, half])
+            step = T // (b + 1)
+            for a in range(0, T, step):
+                cols = slice(a, a + step)
+                nc.vector.tensor_add(res[:, cols], parts[0][:, cols], parts[1][:, cols])
+                nc.sync.dma_start(out=out[b * P : (b + 1) * P, cols], in_=res[:, cols])
 
         nc.sync.dma_start(out=offs_sb[:], in_=offs)
+        pump()
         g0 = take_x(0, V)
         g1 = take_x(1, S)
         quantize_x(0, g0)
@@ -248,24 +277,30 @@ def tile_routed_moe_kernel(tc, xT, w1, w2, gate, offs, pos1, pos2, out):
         gather_words(0, 0)
         quantize_x(1, g1)
         quantize_x(2, g2)
-        gather_words(1, 0)
-        gather_words(2, 0)
+        gather_words(0, 1)
+        gather_words(0, 2)
         gather_bytes(0)
-
-        later = []
-        for i in (1, 2):
-            later += [lambda c=c, i=i: gather_words(c, i) for c in range(PASSES)]
-            later.append(lambda i=i: gather_bytes(i))
 
         for e in range(E):
             last = e == E - 1
-            g01 = groups.tile([P, 2 * H * PACK], BF16, name="group01", align_bytes=64, bufs=3)
-            permuted(g01[:, 0 : H * PACK], take(("w1", e, 0))[:], S)
+            found = {}
+            for group in W1_LOADS[e]:
+                for c in group:
+                    found[c] = (("w1", (e, group[0]), len(group)), c - group[0])
+
+            def interleave(c, group, shares):
+                item, at = found[c]
+                permuted(group, raw[item][:, at], shares)
+                if at == item[2] - 1:
+                    done(item)
+
+            g01 = groups.tile([P, 2 * H * PACK], BF16, name="group01", align_bytes=64, bufs=2)
+            interleave(0, g01[:, 0 : H * PACK], S)
             if e > 0:
                 activate(e - 1)
-            permuted(g01[:, H * PACK :], take(("w1", e, 1))[:], V)
-            if later:
-                later.pop(0)()
+            interleave(1, g01[:, H * PACK :], V)
+            if e % 2 == 0 and e < 6:
+                gather_some(e // 2 + 1, 0)
             w01 = quantize(g01, 2 * H, "w01", 3)
             if e > 0:
                 quantize_h(e - 1)
@@ -273,12 +308,12 @@ def tile_routed_moe_kernel(tc, xT, w1, w2, gate, offs, pos1, pos2, out):
                 layer2(0)
                 layer2(1)
             g_2 = groups.tile([P, H * PACK], BF16, name="group", align_bytes=64, bufs=4)
-            permuted(g_2[:], take(("w1", e, 2))[:], VS if last else S)
+            interleave(2, g_2[:], VS if last else SV)
             if e == 1:
                 gw = take_w2(0, V)
                 quantize_w2(0, gw)
-            if later:
-                later.pop(0)()
+            if e % 2 == 0 and e < 6:
+                gather_some(e // 2 + 1, 1)
             w_2 = quantize(g_2, H, "w_2", 3)
             layer1(e, w01, w_2)
 
@@ -292,11 +327,11 @@ def tile_routed_moe_kernel(tc, xT, w1, w2, gate, offs, pos1, pos2, out):
         quantize_h(7)
         layer2(4)
         layer2(5)
-        gb = take_w2(3, S)
-        gc = take_w2(4, V)
-        quantize_w2(3, gb)
+        g6 = take_late(6, (S, S))
+        g7 = take_late(7, (V, S))
+        quantize_late(6, g6)
         layer2(6)
-        quantize_w2(4, gc)
+        quantize_late(7, g7)
         layer2(7)
         for b in range(2):
             combine(b)

from contextlib import ExitStack

import concourse.mybir as mybir

K, T, E, C, H, N = 1536, 512, 8, 128, 512, 256
P = 128
PACK = 4
K_PASS = P * PACK
PASSES = K // K_PASS
SLOTS = E * C
FLOPS = 2 * SLOTS * (K * H + H * N)

F32 = mybir.dt.float32
BF16 = mybir.dt.bfloat16
U32 = mybir.dt.uint32
U16 = mybir.dt.uint16
U8 = mybir.dt.uint8
FP8X4 = mybir.dt.float8_e4m3fn_x4
MULT = mybir.AluOpType.mult
GELU = mybir.ActivationFunctionType.Gelu_apprx_tanh

CHUNK = 256
W1_LOADS = tuple(((0,), (1,), (2,)) for e in range(E))
W2_PAIRS = ((0, 1), (2, 3), (4, 5))
RINGS = {1: 10}
IN_FLIGHT = 8
Y_GROUPS = ((0, 1, 2, 3), (4, 5), (6,), (7,))


def tile_routed_moe_kernel(tc, xT, w1, w2, gate, offs, pos1, pos2, out):
    nc = tc.nc
    with ExitStack() as ctx:
        lists = ctx.enter_context(tc.tile_pool(name="lists", bufs=1))
        keep = ctx.enter_context(tc.tile_pool(name="keep", bufs=1))
        raws = ctx.enter_context(tc.tile_pool(name="raws", bufs=2))
        groups = ctx.enter_context(tc.tile_pool(name="groups", bufs=3))
        wcodes = ctx.enter_context(tc.tile_pool(name="wcodes", bufs=3))
        slots = ctx.enter_context(tc.tile_pool(name="slots", bufs=2))
        small = ctx.enter_context(tc.tile_pool(name="small", bufs=3))
        psum = ctx.enter_context(tc.psum_pool(name="psum", bufs=3))
        psum_y = ctx.enter_context(tc.psum_pool(name="psum_y", bufs=2))

        offs_sb = lists.tile([P, SLOTS // 16], U16, name="offs_sb")
        pos1_sb = lists.tile([P, T // 16], U16, name="pos1_sb")
        pos2_sb = lists.tile([P, T // 16], U16, name="pos2_sb")

        tok_codes = [keep.tile([P, T], U32, name=f"tok_codes{c}", align_bytes=64) for c in range(PASSES)]
        tok_scales = keep.tile([P, T], U8, name="tok_scales", align_bytes=64)
        y = [keep.tile([P, SLOTS], F32, name=f"y{b}") for b in range(2)]
        gates = [keep.tile([P, 2, T], F32, name=f"gate{b}") for b in range(2)]
        warm = keep.tile([P, 8], F32, name="warm")

        nc.gpsimd.memset(tok_scales[:], 0)
        nc.vector.memset(warm[:], 0.0)
        nc.scalar.activation(warm[:], warm[:], GELU)

        items = [("x", c, 1) for c in range(PASSES)]
        for e in range(E):
            items += [("w1", (e, group[0]), len(group)) for group in W1_LOADS[e]]
            if e == 1:
                items.append(("w2", 0, 1))
        items += [("w2", 1, 1), ("w2", 2, 1)]
        items += [("late", e, 1) for e in (E - 2, E - 1)]
        items += [("gate", b, 1) for b in range(2)]

        raw = {}
        room = dict(RINGS)
        room["late"] = 2
        room["gate"] = 2

        def ring_of(item):
            return item[0] if item[0] in ("late", "gate") else item[2]

        def load(item):
            kind, which, size = item
            if kind == "x":
                t = raws.tile([P, 1, PACK, T], F32, name="raw1", bufs=RINGS[1])
                src = xT[which * K_PASS : (which + 1) * K_PASS, :].rearrange("(g p j) n -> p g j n", p=P, j=PACK)
            elif kind == "w1":
                e, c = which
                t = raws.tile([P, size, PACK, H], F32, name=f"raw{size}", bufs=RINGS[size])
                src = w1[e, c * K_PASS : (c + size) * K_PASS, :].rearrange("(g p j) n -> p g j n", p=P, j=PACK)
            elif kind == "w2":
                t = raws.tile([P, 2, PACK, N], F32, name="raw1", bufs=RINGS[1])
                src = w2[2 * which : 2 * which + 2].rearrange("x (p j) n -> p x j n", j=PACK)
            elif kind == "late":
                t = raws.tile([P, PACK, N], F32, name="raw_late")
                src = w2[which].rearrange("(p j) n -> p j n", j=PACK)
            else:
                t = gates[which]
                src = gate[:, which * P : (which + 1) * P, :].rearrange("r n t -> n r t")
            nc.sync.dma_start(out=t[:], in_=src)
            raw[item] = t
            if item == ("x", PASSES - 1, 1):
                nc.sync.dma_start(out=pos1_sb[:], in_=pos1)
                nc.sync.dma_start(out=pos2_sb[:], in_=pos2)

        def pump():
            while items and room[ring_of(items[0])] > 0 and len(raw) < IN_FLIGHT:
                item = items.pop(0)
                room[ring_of(item)] -= 1
                load(item)

        def done(item):
            raw.pop(item)
            room[ring_of(item)] += 1
            pump()

        def share(dst, src, units, shares):
            at = 0
            for engine, part in shares:
                end = at + part * units // 8
                if engine == "v":
                    nc.vector.tensor_copy(out=dst[:, at:end], in_=src[:, at:end])
                else:
                    nc.scalar.copy(out=dst[:, at:end], in_=src[:, at:end])
                at = end

        def plain(group, raw_tile, width, shares):
            share(
                group.rearrange("p (n i j) -> p n j i", i=4, j=PACK),
                raw_tile.rearrange("p j (n i) -> p n j i", i=4),
                width // 4,
                shares,
            )

        def permuted(group, raw_tile, shares):
            share(
                group.rearrange("p (t m j) -> p m j t", t=PACK, j=PACK),
                raw_tile.rearrange("p j (m t) -> p m j t", t=PACK),
                P,
                shares,
            )

        V, S, VS, SV = [("v", 8)], [("s", 8)], [("v", 5), ("s", 3)], [("v", 3), ("s", 5)]

        def take_x(c, shares):
            item = ("x", c, 1)
            g = groups.tile([P, T * PACK], BF16, name="group", align_bytes=64, bufs=4)
            plain(g[:], raw[item][:, 0], T, shares)
            done(item)
            return g

        def quantize_x(c, g):
            nc.vector.quantize_mx(out=tok_codes[c][:].bitcast(FP8X4), scales=tok_scales[4 * c : P, :], in_=g[:])

        def quantize(g, width, name, bufs):
            w = wcodes.tile([P, width], U32, name=name + "_codes", align_bytes=64, bufs=bufs)
            s = wcodes.tile([P, width], U8, name=name + "_scales", align_bytes=64, bufs=bufs)
            nc.vector.quantize_mx(out=w[:].bitcast(FP8X4), scales=s[:], in_=g[:])
            return w, s

        slot_words = {}
        slot_bytes = {}

        def gather_words(i, c):
            if c == 0:
                slot_words[i] = slots.tile([P, PASSES, CHUNK], U32, name="slot_words", align_bytes=64)
            at = offs_sb[:, i * CHUNK // 16 : (i + 1) * CHUNK // 16]
            nc.vector.tensor_copy(out=slot_words[i][:, c, :], in_=tok_codes[c][:].indirect(at))

        def gather_bytes(i):
            slot_bytes[i] = slots.tile([P, CHUNK], U8, name="slot_bytes", align_bytes=64)
            at = offs_sb[:, i * CHUNK // 16 : (i + 1) * CHUNK // 16]
            nc.vector.tensor_copy(out=slot_bytes[i][:], in_=tok_scales[:].indirect(at))

        def gather_some(i, part):
            if part == 0:
                gather_words(i, 0)
                gather_words(i, 1)
            else:
                gather_words(i, 2)
                gather_bytes(i)

        w2_codes = {}

        def take_w2(i, shares):
            item = ("w2", i, 1)
            g = groups.tile([P, 2 * N * PACK], BF16, name="group", align_bytes=64, bufs=4)
            for x in range(2):
                plain(g[:, x * N * PACK : (x + 1) * N * PACK], raw[item][:, x], N, shares)
            done(item)
            return g

        def quantize_w2(i, g):
            pair = quantize(g, 2 * N, "w2pair", 3)
            for x, e in enumerate(W2_PAIRS[i]):
                w2_codes[e] = [(pair, x * N + b * P) for b in range(2)]

        def take_late(e, shares):
            item = ("late", e, 1)
            halves = []
            for b in range(2):
                g = groups.tile([P, P * PACK], BF16, name="group_half", align_bytes=64, bufs=4)
                plain(g[:], raw[item][:, :, b * P : (b + 1) * P], P, shares[b])
                halves.append(g)
            done(item)
            return halves

        def quantize_late(e, halves):
            w2_codes[e] = [(quantize(g, P, "w2half", 4), 0) for g in halves]

        sums = {}
        hidden = {}
        hcodes = {}
        banks = {}

        def layer1(e, w01, w_2):
            acc = psum.tile([P, PACK, C], F32, name="acc")
            cols = slice((e % 2) * C, (e % 2 + 1) * C)
            for t in range(PACK):
                for c in range(PASSES):
                    w, s = w01 if c < 2 else w_2
                    lo = (c % 2) * H + t * P
                    nc.tensor.matmul_mx(
                        out=acc[:, t, :],
                        lhsT=w[:, lo : lo + P].bitcast(FP8X4),
                        lhsT_scale=s[:, lo : lo + P],
                        rhs=slot_words[e // 2][:, c, cols].bitcast(FP8X4),
                        rhs_scale=slot_bytes[e // 2][4 * c : P, cols],
                        start=(c == 0),
                        stop=(c == PASSES - 1),
                    )
            sums[e] = acc

        def activate(e):
            h = small.tile([P, C, PACK], BF16, name="h", align_bytes=64)
            nc.scalar.activation(h[:], sums.pop(e)[:].rearrange("p t n -> p n t"), GELU)
            hidden[e] = h

        def quantize_h(e):
            h = hidden.pop(e)
            w = small.tile([P, C], U32, name="h_codes", align_bytes=64, bufs=8)
            s = small.tile([P, C], U8, name="h_scales", align_bytes=64, bufs=8)
            nc.vector.quantize_mx(out=w[:].bitcast(FP8X4), scales=s[:], in_=h[:].rearrange("p n t -> p (n t)"))
            hcodes[e] = (w, s)

        def layer2(e):
            group = [g for g in Y_GROUPS if e in g][0]
            hw, hs = hcodes[e]
            at = (e - group[0]) * C
            for b in range(2):
                if e == group[0]:
                    banks[b] = psum_y.tile([P, 4 * C], F32, name=f"bank{b}")
                (w, s), lo = w2_codes[e][b]
                nc.tensor.matmul_mx(
                    out=banks[b][:, at : at + C],
                    lhsT=w[:, lo : lo + P].bitcast(FP8X4),
                    lhsT_scale=s[:, lo : lo + P],
                    rhs=hw[:].bitcast(FP8X4),
                    rhs_scale=hs[:],
                    start=True,
                    stop=True,
                )
                if e == group[-1]:
                    nc.scalar.copy(out=y[b][:, group[0] * C : (e + 1) * C], in_=banks[b][:, 0 : len(group) * C])

        def combine(b):
            parts = []
            for r, plist in ((0, pos1_sb), (1, pos2_sb)):
                part = small.tile([P, T], F32, name=f"part{r}", bufs=2)
                nc.vector.tensor_tensor(part[:], y[b][:].indirect(plist[:]), gates[b][:, r, :], MULT)
                parts.append(part)
            res = small.tile([P, T], F32, name="res", bufs=2)
            step = T // (b + 1)
            for a in range(0, T, step):
                cols = slice(a, a + step)
                nc.vector.tensor_add(res[:, cols], parts[0][:, cols], parts[1][:, cols])
                nc.sync.dma_start(out=out[b * P : (b + 1) * P, cols], in_=res[:, cols])

        nc.sync.dma_start(out=offs_sb[:], in_=offs)
        pump()
        g0 = take_x(0, V)
        g1 = take_x(1, S)
        quantize_x(0, g0)
        g2 = take_x(2, VS)
        gather_words(0, 0)
        quantize_x(1, g1)
        quantize_x(2, g2)
        gather_words(0, 1)
        gather_words(0, 2)
        gather_bytes(0)

        for e in range(E):
            last = e == E - 1
            found = {}
            for group in W1_LOADS[e]:
                for c in group:
                    found[c] = (("w1", (e, group[0]), len(group)), c - group[0])

            def interleave(c, group, shares):
                item, at = found[c]
                permuted(group, raw[item][:, at], shares)
                if at == item[2] - 1:
                    done(item)

            g01 = groups.tile([P, 2 * H * PACK], BF16, name="group01", align_bytes=64, bufs=2)
            interleave(0, g01[:, 0 : H * PACK], S)
            if e > 0:
                activate(e - 1)
            interleave(1, g01[:, H * PACK :], V)
            if e % 2 == 0 and e < 6:
                gather_some(e // 2 + 1, 0)
            w01 = quantize(g01, 2 * H, "w01", 3)
            if e > 0:
                quantize_h(e - 1)
            if e == 2:
                layer2(0)
                layer2(1)
            g_2 = groups.tile([P, H * PACK], BF16, name="group", align_bytes=64, bufs=4)
            interleave(2, g_2[:], VS if last else SV)
            if e == 1:
                gw = take_w2(0, V)
                quantize_w2(0, gw)
            if e % 2 == 0 and e < 6:
                gather_some(e // 2 + 1, 1)
            w_2 = quantize(g_2, H, "w_2", 3)
            layer1(e, w01, w_2)

        ga = take_w2(1, VS)
        gb = take_w2(2, V)
        quantize_w2(1, ga)
        layer2(2)
        layer2(3)
        activate(7)
        quantize_w2(2, gb)
        quantize_h(7)
        layer2(4)
        layer2(5)
        g6 = take_late(6, (S, S))
        g7 = take_late(7, (V, S))
        quantize_late(6, g6)
        layer2(6)
        quantize_late(7, g7)
        layer2(7)
        for b in range(2):
            combine(b)
